import numpy as np
import ml_dtypes


def mxq(x, axis, fmt="e4m3"):
    dtype, down = {"e4m3": (ml_dtypes.float8_e4m3fn, 7), "e5m2": (ml_dtypes.float8_e5m2, 14)}[fmt]
    v = np.moveaxis(np.asarray(x, np.float32).astype(ml_dtypes.bfloat16).astype(np.float64), axis, -1)
    blocks = v.reshape(v.shape[:-1] + (-1, 32))
    amax = np.abs(blocks).max(-1, keepdims=True)
    byte = np.maximum(np.where(amax > 0, np.frexp(amax)[1] - 1 + 127, 0) - down, 1)
    scale = np.exp2(byte - 127.0)
    codes = (blocks / scale).astype(np.float32).astype(dtype).astype(np.float64)
    return np.moveaxis((codes * scale).reshape(v.shape), -1, axis)


WIDE = False


def mx_kscale(k):
    if not WIDE:
        return np.ones(k)
    levels = np.array([10, -10, 5, -5, 0])
    if k % 512:
        return np.exp2(np.random.permutation(np.resize(levels, k // 32))).repeat(32)
    a = np.empty((k // 512, 16))
    for p in range(k // 512):
        a[p, :8] = np.random.permutation(np.resize(levels, 8))
        for g in range(8):
            far = levels[np.abs(levels - a[p, g]) >= 10]
            a[p, g + 8] = far[np.random.randint(len(far))]
    return np.exp2(a.ravel()).repeat(32)


def f64(x):
    return np.asarray(x).astype(np.float64)


def striped(idx):
    return np.tile(idx.reshape(-1, 16).T, (8, 1)).astype(np.uint16)


def unstriped(offs):
    return offs[:16].T.reshape(-1).astype(np.int64)


def pack_weight(w):
    k, n = w.shape
    w = f64(np.asarray(w, np.float32).astype(ml_dtypes.bfloat16)).reshape(k // 32, 32, n)
    amax = np.abs(w).max(1)
    byte = np.clip(np.where(amax > 0, np.frexp(amax)[1] - 1 + 127 - 7, 1), 1, 254)
    scaled = (w * np.exp2(127.0 - byte)[:, None, :]).reshape(k, n).astype(np.float32)
    words = np.ascontiguousarray(scaled.reshape(k // 512, 128, 4, n).transpose(0, 1, 3, 2)).astype(ml_dtypes.float8_e4m3fn).view(np.uint8)
    return words, np.ascontiguousarray(byte.astype(np.uint8).reshape(k // 512, 16, n))


def unpack_weight(words, scales):
    g, p, n, _ = words.shape
    vals = np.ascontiguousarray(words).view(ml_dtypes.float8_e4m3fn).astype(np.float64) * np.repeat(np.exp2(scales.astype(np.float64) - 127.0), 8, axis=1)[..., None]
    return vals.transpose(0, 1, 3, 2).reshape(g * 512, n)


def relu(v):
    return np.maximum(v, 0.0)


K, T, S, N = 1024, 256, 512, 2048


def setup_inputs():
    n = np.random.standard_normal
    s = mx_kscale(K)[:, None]
    packed = pack_weight(n((K, N)) / np.sqrt(K) / s)
    return {
        "w_words": packed[0],
        "w_scales": packed[1],
        "xT": (n((K, T)) * s).astype(np.float32),
        "b": (0.3 * n((S, 1))).astype(np.float32),
        "offs": striped(np.sort(np.random.permutation(N)[:S])),
    }


def reference(w_words, w_scales, xT, b, offs):
    idx = unstriped(offs)
    wq = unpack_weight(w_words, w_scales)[:, idx]
    return relu((wq.T @ mxq(f64(xT), 0, "e4m3")) + f64(b))

@@ -1,0 +1,112 @@
+from contextlib import ExitStack
+
+import concourse.mybir as mybir
+from concourse.masks import make_identity
+
+K, T, S, N = 1024, 256, 512, 2048
+FLOPS = 2 * K * T * S
+
+F32 = mybir.dt.float32
+BF16 = mybir.dt.bfloat16
+I32 = mybir.dt.int32
+U32 = mybir.dt.uint32
+U16 = mybir.dt.uint16
+U8 = mybir.dt.uint8
+FP8X4 = mybir.dt.float8_e4m3fn_x4
+ACT = mybir.ActivationFunctionType
+ALU = mybir.AluOpType
+
+P = 128
+PACK = 4
+K_PASS = P * PACK
+PASSES = K // K_PASS
+TILES = S // P
+HALF = S // 2
+LIST_ROWS = 16
+REACH = N - HALF
+
+
+def tile_picked_neuron_lin_relu_srt_p_kernel(tc, w_words, w_scales, xT, b, offs, out):
+    nc = tc.nc
+    with ExitStack() as ctx:
+        keep = ctx.enter_context(tc.tile_pool(name="keep", bufs=1))
+        psum = ctx.enter_context(tc.psum_pool(name="psum", bufs=1))
+
+        offsets = keep.tile([P, S // LIST_ROWS], U16, name="offsets")
+        x_raw = [keep.tile([P, PACK, T], F32, name=f"x_raw{o}") for o in range(PASSES)]
+        words = [keep.tile([P, N], I32, name=f"words{o}", align_bytes=64) for o in range(PASSES)]
+        scale_rows = keep.tile([P, N], U8, name="scale_rows", tag="scale_rows_then_picked", align_bytes=64)
+        bias_rows = keep.tile([P, P], F32, name="bias_rows")
+        identity = keep.tile([P, P], F32, name="identity")
+
+        make_identity(nc, identity[:])
+        nc.vector.memset(scale_rows[:].bitcast(I32), 0)
+        nc.vector.memset(bias_rows[:], 0.0)
+
+        for o in range(PASSES):
+            rows = xT[o * K_PASS : (o + 1) * K_PASS, :]
+            nc.sync.dma_start(out=x_raw[o][:], in_=rows.rearrange("(p j) t -> p j t", j=PACK))
+        nc.sync.dma_start(offsets[:], offs)
+        w_rows = [w_words[o].rearrange("p n r -> p (n r)").bitcast(I32) for o in range(PASSES)]
+        nc.sync.dma_start(out=words[0][:], in_=w_rows[0])
+        nc.sync.dma_start(out=words[1][:, :REACH], in_=w_rows[1][:, :REACH])
+        nc.sync.dma_start(out=words[1][:, REACH:], in_=w_rows[1][:, REACH:])
+
+        for q in range(4):
+            nc.gpsimd.dma_start(
+                out=scale_rows[32 * q : 32 * q + 4 * PASSES, :].bitcast(I32),
+                in_=w_scales.bitcast(I32)[:, 4 * q : 4 * q + 4, :],
+            )
+        nc.scalar.dma_start(out=bias_rows[0:TILES, :], in_=b.rearrange("(m p) one -> m (p one)", p=P))
+
+        bias_turned = psum.tile([P, P], F32, name="bias_turned")
+        nc.tensor.transpose(bias_turned[:], bias_rows[:], identity[:])
+        bias = keep.tile([P, TILES], F32, name="bias")
+        nc.scalar.copy(bias[:], bias_turned[:, 0:TILES])
+
+        x_codes = []
+        x_scales = []
+        for o in range(PASSES):
+            grouped = keep.tile([P, T, PACK], BF16, name=f"grouped{o}", align_bytes=64)
+            if o == 0:
+                nc.scalar.copy(grouped[:], x_raw[o][:].rearrange("p j t -> p t j"))
+            else:
+                nc.vector.tensor_copy(grouped[:], x_raw[o][:].rearrange("p j t -> p t j"))
+            codes = keep.tile([P, T], U32, name=f"x_codes{o}", align_bytes=64)
+            scales = keep.tile([P, T], U8, name=f"x_scales{o}", align_bytes=64)
+            nc.vector.quantize_mx(
+                out=codes[:].bitcast(FP8X4), scales=scales[:], in_=grouped[:].rearrange("p t j -> p (t j)")
+            )
+            x_codes.append(codes)
+            x_scales.append(scales)
+
+        picked_scales = keep.tile([P, S], U8, name="picked_scales", align_bytes=64)
+        nc.vector.tensor_copy(picked_scales[:], scale_rows[:].indirect(offsets[:]))
+
+        acc = [psum.tile([P, T], F32, name=f"acc{m}") for m in range(TILES)]
+        for o in range(PASSES):
+            for h in range(2):
+                tag = "scale_rows_then_picked" if (o, h) == (1, 0) else f"picked{o}_{h}"
+                picked = keep.tile([P, HALF], U32, name=f"picked{o}_{h}", tag=tag, align_bytes=64)
+                reach = REACH if h == 0 else N
+                cols = slice(h * HALF // LIST_ROWS, (h + 1) * HALF // LIST_ROWS)
+                nc.vector.tensor_copy(picked[:], words[o][:, :reach].bitcast(U32).indirect(offsets[:, cols]))
+                for i in range(HALF // P):
+                    m = h * (HALF // P) + i
+                    nc.tensor.matmul_mx(
+                        out=acc[m][:],
+                        lhsT=picked[:, i * P : (i + 1) * P].bitcast(FP8X4),
+                        lhsT_scale=picked_scales[4 * o :, m * P : (m + 1) * P],
+                        rhs=x_codes[o][:].bitcast(FP8X4),
+                        rhs_scale=x_scales[o][:],
+                        start=(o == 0),
+                        stop=(o == PASSES - 1),
+                    )
+
+        for m in range(TILES):
+            result = keep.tile([P, T], F32, name=f"result{m}")
+            if m < TILES - 1:
+                nc.scalar.activation(result[:], acc[m][:], ACT.Relu, bias=bias[:, m : m + 1])
+            else:
+                nc.vector.tensor_scalar(result[:], acc[m][:], bias[:, m : m + 1], 0.0, ALU.add, ALU.max)
+            nc.sync.dma_start(out=out[m * P : (m + 1) * P, :], in_=result[:])

@@ -33,7 +33,7 @@ def tile_picked_neuron_lin_relu_srt_p_kernel(tc, w_words, w_scales, xT, b, offs,
         psum = ctx.enter_context(tc.psum_pool(name="psum", bufs=1))
 
         offsets = keep.tile([P, S // LIST_ROWS], U16, name="offsets")
-        x_raw = [keep.tile([P, PACK, T], F32, name=f"x_raw{o}") for o in range(PASSES)]
+        x_raw = keep.tile([P, PASSES, PACK, T], F32, name="x_raw")
         words = [keep.tile([P, N], I32, name=f"words{o}", align_bytes=64) for o in range(PASSES)]
         scale_rows = keep.tile([P, N], U8, name="scale_rows", tag="scale_rows_then_picked", align_bytes=64)
         bias_rows = keep.tile([P, P], F32, name="bias_rows")
@@ -43,17 +43,15 @@ def tile_picked_neuron_lin_relu_srt_p_kernel(tc, w_words, w_scales, xT, b, offs,
         nc.vector.memset(scale_rows[:].bitcast(I32), 0)
         nc.vector.memset(bias_rows[:], 0.0)
 
-        for o in range(PASSES):
-            rows = xT[o * K_PASS : (o + 1) * K_PASS, :]
-            nc.sync.dma_start(out=x_raw[o][:], in_=rows.rearrange("(p j) t -> p j t", j=PACK))
         nc.sync.dma_start(offsets[:], offs)
+        nc.sync.dma_start(out=x_raw[:], in_=xT.rearrange("(o p j) t -> p o j t", o=PASSES, j=PACK))
         w_rows = [w_words[o].rearrange("p n r -> p (n r)").bitcast(I32) for o in range(PASSES)]
         nc.sync.dma_start(out=words[0][:], in_=w_rows[0])
         nc.sync.dma_start(out=words[1][:, :REACH], in_=w_rows[1][:, :REACH])
         nc.sync.dma_start(out=words[1][:, REACH:], in_=w_rows[1][:, REACH:])
 
         for q in range(4):
-            nc.gpsimd.dma_start(
+            nc.scalar.dma_start(
                 out=scale_rows[32 * q : 32 * q + 4 * PASSES, :].bitcast(I32),
                 in_=w_scales.bitcast(I32)[:, 4 * q : 4 * q + 4, :],
             )
@@ -69,9 +67,9 @@ def tile_picked_neuron_lin_relu_srt_p_kernel(tc, w_words, w_scales, xT, b, offs,
         for o in range(PASSES):
             grouped = keep.tile([P, T, PACK], BF16, name=f"grouped{o}", align_bytes=64)
             if o == 0:
-                nc.scalar.copy(grouped[:], x_raw[o][:].rearrange("p j t -> p t j"))
+                nc.scalar.copy(grouped[:], x_raw[:, o].rearrange("p j t -> p t j"))
             else:
-                nc.vector.tensor_copy(grouped[:], x_raw[o][:].rearrange("p j t -> p t j"))
+                nc.vector.tensor_copy(grouped[:], x_raw[:, o].rearrange("p j t -> p t j"))
             codes = keep.tile([P, T], U32, name=f"x_codes{o}", align_bytes=64)
             scales = keep.tile([P, T], U8, name=f"x_scales{o}", align_bytes=64)
             nc.vector.quantize_mx(

@@ -44,17 +44,19 @@ def tile_picked_neuron_lin_relu_srt_p_kernel(tc, w_words, w_scales, xT, b, offs,
         nc.vector.memset(bias_rows[:], 0.0)
 
         nc.sync.dma_start(offsets[:], offs)
-        nc.sync.dma_start(out=x_raw[:], in_=xT.rearrange("(o p j) t -> p o j t", o=PASSES, j=PACK))
+        x_rows = xT.rearrange("(o p j) t -> p o j t", o=PASSES, j=PACK)
+        for o in range(PASSES):
+            nc.sync.dma_start(out=x_raw[:, o], in_=x_rows[:, o])
+        for q in range(4):
+            nc.sync.dma_start(
+                out=scale_rows[32 * q : 32 * q + 4 * PASSES, :].bitcast(I32),
+                in_=w_scales.bitcast(I32)[:, 4 * q : 4 * q + 4, :],
+            )
         w_rows = [w_words[o].rearrange("p n r -> p (n r)").bitcast(I32) for o in range(PASSES)]
         nc.sync.dma_start(out=words[0][:], in_=w_rows[0])
         nc.sync.dma_start(out=words[1][:, :REACH], in_=w_rows[1][:, :REACH])
         nc.sync.dma_start(out=words[1][:, REACH:], in_=w_rows[1][:, REACH:])
 
-        for q in range(4):
-            nc.scalar.dma_start(
-                out=scale_rows[32 * q : 32 * q + 4 * PASSES, :].bitcast(I32),
-                in_=w_scales.bitcast(I32)[:, 4 * q : 4 * q + 4, :],
-            )
         nc.scalar.dma_start(out=bias_rows[0:TILES, :], in_=b.rearrange("(m p) one -> m (p one)", p=P))
 
         bias_turned = psum.tile([P, P], F32, name="bias_turned")
@@ -103,7 +105,7 @@ def tile_picked_neuron_lin_relu_srt_p_kernel(tc, w_words, w_scales, xT, b, offs,
 
         for m in range(TILES):
             result = keep.tile([P, T], F32, name=f"result{m}")
-            if m < TILES - 1:
+            if m % 2 == 0:
                 nc.scalar.activation(result[:], acc[m][:], ACT.Relu, bias=bias[:, m : m + 1])
             else:
                 nc.vector.tensor_scalar(result[:], acc[m][:], bias[:, m : m + 1], 0.0, ALU.add, ALU.max)

@@ -43,20 +43,26 @@ def tile_picked_neuron_lin_relu_srt_p_kernel(tc, w_words, w_scales, xT, b, offs,
         nc.vector.memset(scale_rows[:].bitcast(I32), 0)
         nc.vector.memset(bias_rows[:], 0.0)
 
-        nc.sync.dma_start(offsets[:], offs)
         x_rows = xT.rearrange("(o p j) t -> p o j t", o=PASSES, j=PACK)
-        for o in range(PASSES):
-            nc.sync.dma_start(out=x_raw[:, o], in_=x_rows[:, o])
-        for q in range(4):
-            nc.sync.dma_start(
-                out=scale_rows[32 * q : 32 * q + 4 * PASSES, :].bitcast(I32),
-                in_=w_scales.bitcast(I32)[:, 4 * q : 4 * q + 4, :],
-            )
+        nc.sync.dma_start(offsets[:], offs)
+        nc.sync.dma_start(out=x_raw[:, 0], in_=x_rows[:, 0])
+        nc.sync.dma_start(out=x_raw[:, 1], in_=x_rows[:, 1])
+
+        def load_scale_rows(half):
+            for i in range(2 * half, 2 * half + 2):
+                for o in range(PASSES):
+                    nc.sync.dma_start(
+                        out=scale_rows[4 * o + i : P : 32, :].bitcast(I32),
+                        in_=w_scales.bitcast(I32)[o, i:16:4, :],
+                    )
+
+        load_scale_rows(0)
         w_rows = [w_words[o].rearrange("p n r -> p (n r)").bitcast(I32) for o in range(PASSES)]
-        nc.sync.dma_start(out=words[0][:], in_=w_rows[0])
+        nc.sync.dma_start(out=words[0][:, :REACH], in_=w_rows[0][:, :REACH])
+        load_scale_rows(1)
+        nc.sync.dma_start(out=words[0][:, REACH:], in_=w_rows[0][:, REACH:])
         nc.sync.dma_start(out=words[1][:, :REACH], in_=w_rows[1][:, :REACH])
         nc.sync.dma_start(out=words[1][:, REACH:], in_=w_rows[1][:, REACH:])
-
         nc.scalar.dma_start(out=bias_rows[0:TILES, :], in_=b.rearrange("(m p) one -> m (p one)", p=P))
 
         bias_turned = psum.tile([P, P], F32, name="bias_turned")
@@ -81,7 +87,6 @@ def tile_picked_neuron_lin_relu_srt_p_kernel(tc, w_words, w_scales, xT, b, offs,
             x_scales.append(scales)
 
         picked_scales = keep.tile([P, S], U8, name="picked_scales", align_bytes=64)
-        nc.vector.tensor_copy(picked_scales[:], scale_rows[:].indirect(offsets[:]))
 
         acc = [psum.tile([P, T], F32, name=f"acc{m}") for m in range(TILES)]
         for o in range(PASSES):
@@ -90,6 +95,10 @@ def tile_picked_neuron_lin_relu_srt_p_kernel(tc, w_words, w_scales, xT, b, offs,
                 picked = keep.tile([P, HALF], U32, name=f"picked{o}_{h}", tag=tag, align_bytes=64)
                 reach = REACH if h == 0 else N
                 cols = slice(h * HALF // LIST_ROWS, (h + 1) * HALF // LIST_ROWS)
+                if o == 0:
+                    nc.vector.tensor_copy(
+                        picked_scales[:, h * HALF : (h + 1) * HALF], scale_rows[:].indirect(offsets[:, cols])
+                    )
                 nc.vector.tensor_copy(picked[:], words[o][:, :reach].bitcast(U32).indirect(offsets[:, cols]))
                 for i in range(HALF // P):
                     m = h * (HALF // P) + i

@@ -88,7 +88,8 @@ def tile_picked_neuron_lin_relu_srt_p_kernel(tc, w_words, w_scales, xT, b, offs,
 
         picked_scales = keep.tile([P, S], U8, name="picked_scales", align_bytes=64)
 
-        acc = [psum.tile([P, T], F32, name=f"acc{m}") for m in range(TILES)]
+        spans = [[(0, T // 2), (T // 2, T)] if m in (0, TILES - 1) else [(0, T)] for m in range(TILES)]
+        acc = [[psum.tile([P, hi - lo], F32, name=f"acc{m}_{lo}") for lo, hi in spans[m]] for m in range(TILES)]
         for o in range(PASSES):
             for h in range(2):
                 tag = "scale_rows_then_picked" if (o, h) == (1, 0) else f"picked{o}_{h}"
@@ -102,20 +103,22 @@ def tile_picked_neuron_lin_relu_srt_p_kernel(tc, w_words, w_scales, xT, b, offs,
                 nc.vector.tensor_copy(picked[:], words[o][:, :reach].bitcast(U32).indirect(offsets[:, cols]))
                 for i in range(HALF // P):
                     m = h * (HALF // P) + i
-                    nc.tensor.matmul_mx(
-                        out=acc[m][:],
-                        lhsT=picked[:, i * P : (i + 1) * P].bitcast(FP8X4),
-                        lhsT_scale=picked_scales[4 * o :, m * P : (m + 1) * P],
-                        rhs=x_codes[o][:].bitcast(FP8X4),
-                        rhs_scale=x_scales[o][:],
-                        start=(o == 0),
-                        stop=(o == PASSES - 1),
-                    )
+                    for bank, (lo, hi) in zip(acc[m], spans[m]):
+                        nc.tensor.matmul_mx(
+                            out=bank[:],
+                            lhsT=picked[:, i * P : (i + 1) * P].bitcast(FP8X4),
+                            lhsT_scale=picked_scales[4 * o :, m * P : (m + 1) * P],
+                            rhs=x_codes[o][:, lo:hi].bitcast(FP8X4),
+                            rhs_scale=x_scales[o][:, lo:hi],
+                            start=(o == 0),
+                            stop=(o == PASSES - 1),
+                        )
 
         for m in range(TILES):
             result = keep.tile([P, T], F32, name=f"result{m}")
-            if m % 2 == 0:
-                nc.scalar.activation(result[:], acc[m][:], ACT.Relu, bias=bias[:, m : m + 1])
-            else:
-                nc.vector.tensor_scalar(result[:], acc[m][:], bias[:, m : m + 1], 0.0, ALU.add, ALU.max)
+            for bank, (lo, hi) in zip(acc[m], spans[m]):
+                if m % 2 == 0:
+                    nc.scalar.activation(result[:, lo:hi], bank[:], ACT.Relu, bias=bias[:, m : m + 1])
+                else:
+                    nc.vector.tensor_scalar(result[:, lo:hi], bank[:], bias[:, m : m + 1], 0.0, ALU.add, ALU.max)
             nc.sync.dma_start(out=out[m * P : (m + 1) * P, :], in_=result[:])

@@ -24,6 +24,7 @@ TILES = S // P
 HALF = S // 2
 LIST_ROWS = 16
 REACH = N - HALF
+LEAD = 512
 
 
 def tile_picked_neuron_lin_relu_srt_p_kernel(tc, w_words, w_scales, xT, b, offs, out):
@@ -34,35 +35,25 @@ def tile_picked_neuron_lin_relu_srt_p_kernel(tc, w_words, w_scales, xT, b, offs,
 
         offsets = keep.tile([P, S // LIST_ROWS], U16, name="offsets")
         x_raw = keep.tile([P, PASSES, PACK, T], F32, name="x_raw")
-        words = [keep.tile([P, N], I32, name=f"words{o}", align_bytes=64) for o in range(PASSES)]
-        scale_rows = keep.tile([P, N], U8, name="scale_rows", tag="scale_rows_then_picked", align_bytes=64)
+        scale_rows = keep.tile([P, N], U8, name="scale_rows", tag="scale_rows_then_words", align_bytes=64)
+        words = [keep.tile([P, N], I32, name="words0", align_bytes=64)]
+        planes = keep.tile([P, PASSES, S], U8, name="planes", align_bytes=64)
         bias_rows = keep.tile([P, P], F32, name="bias_rows")
         identity = keep.tile([P, P], F32, name="identity")
 
         make_identity(nc, identity[:])
-        nc.vector.memset(scale_rows[:].bitcast(I32), 0)
         nc.vector.memset(bias_rows[:], 0.0)
+        nc.vector.memset(scale_rows[32:64, :].bitcast(I32), 0)
+        nc.vector.memset(scale_rows[64:P, :].bitcast(I32), 0)
+        nc.vector.memset(planes[:].bitcast(I32), 0)
 
         x_rows = xT.rearrange("(o p j) t -> p o j t", o=PASSES, j=PACK)
+        w_rows = [w_words[o].rearrange("p n r -> p (n r)").bitcast(I32) for o in range(PASSES)]
         nc.sync.dma_start(offsets[:], offs)
+        nc.sync.dma_start(out=scale_rows[0:32, :].bitcast(I32), in_=w_scales.bitcast(I32).rearrange("o q n -> q o n"))
         nc.sync.dma_start(out=x_raw[:, 0], in_=x_rows[:, 0])
         nc.sync.dma_start(out=x_raw[:, 1], in_=x_rows[:, 1])
-
-        def load_scale_rows(half):
-            for i in range(2 * half, 2 * half + 2):
-                for o in range(PASSES):
-                    nc.sync.dma_start(
-                        out=scale_rows[4 * o + i : P : 32, :].bitcast(I32),
-                        in_=w_scales.bitcast(I32)[o, i:16:4, :],
-                    )
-
-        load_scale_rows(0)
-        w_rows = [w_words[o].rearrange("p n r -> p (n r)").bitcast(I32) for o in range(PASSES)]
-        nc.sync.dma_start(out=words[0][:, :REACH], in_=w_rows[0][:, :REACH])
-        load_scale_rows(1)
-        nc.sync.dma_start(out=words[0][:, REACH:], in_=w_rows[0][:, REACH:])
-        nc.sync.dma_start(out=words[1][:, :REACH], in_=w_rows[1][:, :REACH])
-        nc.sync.dma_start(out=words[1][:, REACH:], in_=w_rows[1][:, REACH:])
+        nc.sync.dma_start(out=words[0][:], in_=w_rows[0])
         nc.scalar.dma_start(out=bias_rows[0:TILES, :], in_=b.rearrange("(m p) one -> m (p one)", p=P))
 
         bias_turned = psum.tile([P, P], F32, name="bias_turned")
@@ -70,14 +61,23 @@ def tile_picked_neuron_lin_relu_srt_p_kernel(tc, w_words, w_scales, xT, b, offs,
         bias = keep.tile([P, TILES], F32, name="bias")
         nc.scalar.copy(bias[:], bias_turned[:, 0:TILES])
 
+        picked_scales = keep.tile([P, S], U8, name="picked_scales", align_bytes=64)
+        nc.vector.tensor_copy(picked_scales[:], scale_rows[:].indirect(offsets[:]))
+        words.append(keep.tile([P, N], I32, name="words1", tag="scale_rows_then_words", align_bytes=64))
+        nc.sync.dma_start(out=words[1][:, :LEAD], in_=w_rows[1][:, :LEAD])
+        for q in range(4):
+            nc.sync.dma_start(
+                out=planes[32 * q : 32 * q + 4].bitcast(I32),
+                in_=picked_scales[8 * q : 8 * q + 8, :].bitcast(I32),
+            )
+        nc.sync.dma_start(out=words[1][:, LEAD:REACH], in_=w_rows[1][:, LEAD:REACH])
+        nc.sync.dma_start(out=words[1][:, REACH:], in_=w_rows[1][:, REACH:])
+
         x_codes = []
         x_scales = []
         for o in range(PASSES):
             grouped = keep.tile([P, T, PACK], BF16, name=f"grouped{o}", align_bytes=64)
-            if o == 0:
-                nc.scalar.copy(grouped[:], x_raw[:, o].rearrange("p j t -> p t j"))
-            else:
-                nc.vector.tensor_copy(grouped[:], x_raw[:, o].rearrange("p j t -> p t j"))
+            nc.vector.tensor_copy(grouped[:], x_raw[:, o].rearrange("p j t -> p t j"))
             codes = keep.tile([P, T], U32, name=f"x_codes{o}", align_bytes=64)
             scales = keep.tile([P, T], U8, name=f"x_scales{o}", align_bytes=64)
             nc.vector.quantize_mx(
@@ -86,20 +86,13 @@ def tile_picked_neuron_lin_relu_srt_p_kernel(tc, w_words, w_scales, xT, b, offs,
             x_codes.append(codes)
             x_scales.append(scales)
 
-        picked_scales = keep.tile([P, S], U8, name="picked_scales", align_bytes=64)
-
         spans = [[(0, T // 2), (T // 2, T)] if m in (0, TILES - 1) else [(0, T)] for m in range(TILES)]
         acc = [[psum.tile([P, hi - lo], F32, name=f"acc{m}_{lo}") for lo, hi in spans[m]] for m in range(TILES)]
         for o in range(PASSES):
             for h in range(2):
-                tag = "scale_rows_then_picked" if (o, h) == (1, 0) else f"picked{o}_{h}"
-                picked = keep.tile([P, HALF], U32, name=f"picked{o}_{h}", tag=tag, align_bytes=64)
-                reach = REACH if h == 0 else N
+                picked = keep.tile([P, HALF], U32, name=f"picked{o}_{h}", align_bytes=64)
+                reach = REACH if (o, h) == (1, 0) else N
                 cols = slice(h * HALF // LIST_ROWS, (h + 1) * HALF // LIST_ROWS)
-                if o == 0:
-                    nc.vector.tensor_copy(
-                        picked_scales[:, h * HALF : (h + 1) * HALF], scale_rows[:].indirect(offsets[:, cols])
-                    )
                 nc.vector.tensor_copy(picked[:], words[o][:, :reach].bitcast(U32).indirect(offsets[:, cols]))
                 for i in range(HALF // P):
                     m = h * (HALF // P) + i
@@ -107,7 +100,7 @@ def tile_picked_neuron_lin_relu_srt_p_kernel(tc, w_words, w_scales, xT, b, offs,
                         nc.tensor.matmul_mx(
                             out=bank[:],
                             lhsT=picked[:, i * P : (i + 1) * P].bitcast(FP8X4),
-                            lhsT_scale=picked_scales[4 * o :, m * P : (m + 1) * P],
+                            lhsT_scale=planes[:, o, m * P : (m + 1) * P],
                             rhs=x_codes[o][:, lo:hi].bitcast(FP8X4),
                             rhs_scale=x_scales[o][:, lo:hi],
                             start=(o == 0),

@@ -24,7 +24,6 @@ TILES = S // P
 HALF = S // 2
 LIST_ROWS = 16
 REACH = N - HALF
-LEAD = 512
 
 
 def tile_picked_neuron_lin_relu_srt_p_kernel(tc, w_words, w_scales, xT, b, offs, out):
@@ -50,13 +49,13 @@ def tile_picked_neuron_lin_relu_srt_p_kernel(tc, w_words, w_scales, xT, b, offs,
         x_rows = xT.rearrange("(o p j) t -> p o j t", o=PASSES, j=PACK)
         w_rows = [w_words[o].rearrange("p n r -> p (n r)").bitcast(I32) for o in range(PASSES)]
         nc.sync.dma_start(offsets[:], offs)
-        nc.sync.dma_start(out=scale_rows[0:32, :].bitcast(I32), in_=w_scales.bitcast(I32).rearrange("o q n -> q o n"))
+        nc.scalar.dma_start(out=scale_rows[0:32, :].bitcast(I32), in_=w_scales.bitcast(I32).rearrange("o q n -> q o n"))
         nc.sync.dma_start(out=x_raw[:, 0], in_=x_rows[:, 0])
         nc.sync.dma_start(out=x_raw[:, 1], in_=x_rows[:, 1])
         nc.sync.dma_start(out=words[0][:], in_=w_rows[0])
         nc.scalar.dma_start(out=bias_rows[0:TILES, :], in_=b.rearrange("(m p) one -> m (p one)", p=P))
 
-        bias_turned = psum.tile([P, P], F32, name="bias_turned")
+        bias_turned = psum.tile([P, P], F32, name="bias_turned", tag="acc3_128")
         nc.tensor.transpose(bias_turned[:], bias_rows[:], identity[:])
         bias = keep.tile([P, TILES], F32, name="bias")
         nc.scalar.copy(bias[:], bias_turned[:, 0:TILES])
@@ -64,13 +63,12 @@ def tile_picked_neuron_lin_relu_srt_p_kernel(tc, w_words, w_scales, xT, b, offs,
         picked_scales = keep.tile([P, S], U8, name="picked_scales", align_bytes=64)
         nc.vector.tensor_copy(picked_scales[:], scale_rows[:].indirect(offsets[:]))
         words.append(keep.tile([P, N], I32, name="words1", tag="scale_rows_then_words", align_bytes=64))
-        nc.sync.dma_start(out=words[1][:, :LEAD], in_=w_rows[1][:, :LEAD])
         for q in range(4):
             nc.sync.dma_start(
                 out=planes[32 * q : 32 * q + 4].bitcast(I32),
                 in_=picked_scales[8 * q : 8 * q + 8, :].bitcast(I32),
             )
-        nc.sync.dma_start(out=words[1][:, LEAD:REACH], in_=w_rows[1][:, LEAD:REACH])
+        nc.sync.dma_start(out=words[1][:, :REACH], in_=w_rows[1][:, :REACH])
         nc.sync.dma_start(out=words[1][:, REACH:], in_=w_rows[1][:, REACH:])
 
         x_codes = []
@@ -86,8 +84,8 @@ def tile_picked_neuron_lin_relu_srt_p_kernel(tc, w_words, w_scales, xT, b, offs,
             x_codes.append(codes)
             x_scales.append(scales)
 
-        spans = [[(0, T // 2), (T // 2, T)] if m in (0, TILES - 1) else [(0, T)] for m in range(TILES)]
-        acc = [[psum.tile([P, hi - lo], F32, name=f"acc{m}_{lo}") for lo, hi in spans[m]] for m in range(TILES)]
+        spans = [[(0, T // 2), (T // 2, T)] for m in range(TILES)]
+        acc = [[psum.tile([P, hi - lo], F32, name=f"acc{m}_{lo}", tag=f"acc{m}_{lo}") for lo, hi in spans[m]] for m in range(TILES)]
         for o in range(PASSES):
             for h in range(2):
                 picked = keep.tile([P, HALF], U32, name=f"picked{o}_{h}", align_bytes=64)
@@ -110,7 +108,7 @@ def tile_picked_neuron_lin_relu_srt_p_kernel(tc, w_words, w_scales, xT, b, offs,
         for m in range(TILES):
             result = keep.tile([P, T], F32, name=f"result{m}")
             for bank, (lo, hi) in zip(acc[m], spans[m]):
-                if m % 2 == 0:
+                if lo == 0:
                     nc.scalar.activation(result[:, lo:hi], bank[:], ACT.Relu, bias=bias[:, m : m + 1])
                 else:
                     nc.vector.tensor_scalar(result[:, lo:hi], bank[:], bias[:, m : m + 1], 0.0, ALU.add, ALU.max)

@@ -24,6 +24,7 @@ TILES = S // P
 HALF = S // 2
 LIST_ROWS = 16
 REACH = N - HALF
+LEAD = 512
 
 
 def tile_picked_neuron_lin_relu_srt_p_kernel(tc, w_words, w_scales, xT, b, offs, out):
@@ -41,41 +42,43 @@ def tile_picked_neuron_lin_relu_srt_p_kernel(tc, w_words, w_scales, xT, b, offs,
         identity = keep.tile([P, P], F32, name="identity")
 
         make_identity(nc, identity[:])
-        nc.vector.memset(bias_rows[:], 0.0)
-        nc.vector.memset(scale_rows[32:64, :].bitcast(I32), 0)
-        nc.vector.memset(scale_rows[64:P, :].bitcast(I32), 0)
+        nc.vector.memset(bias_rows[: P - TILES, :], 0.0)
+        nc.vector.memset(scale_rows[:96, :].bitcast(I32), 0)
         nc.vector.memset(planes[:].bitcast(I32), 0)
 
         x_rows = xT.rearrange("(o p j) t -> p o j t", o=PASSES, j=PACK)
         w_rows = [w_words[o].rearrange("p n r -> p (n r)").bitcast(I32) for o in range(PASSES)]
         nc.sync.dma_start(offsets[:], offs)
-        nc.scalar.dma_start(out=scale_rows[0:32, :].bitcast(I32), in_=w_scales.bitcast(I32).rearrange("o q n -> q o n"))
-        nc.sync.dma_start(out=x_raw[:, 0], in_=x_rows[:, 0])
-        nc.sync.dma_start(out=x_raw[:, 1], in_=x_rows[:, 1])
+        nc.sync.dma_start(out=scale_rows[96:, :].bitcast(I32), in_=w_scales.bitcast(I32).rearrange("o q n -> q o n"))
+        nc.sync.dma_start(out=x_raw[:], in_=x_rows)
         nc.sync.dma_start(out=words[0][:], in_=w_rows[0])
-        nc.scalar.dma_start(out=bias_rows[0:TILES, :], in_=b.rearrange("(m p) one -> m (p one)", p=P))
+        nc.scalar.dma_start(out=bias_rows[P - TILES :, :], in_=b.rearrange("(m p) one -> m (p one)", p=P))
 
         bias_turned = psum.tile([P, P], F32, name="bias_turned", tag="acc3_128")
         nc.tensor.transpose(bias_turned[:], bias_rows[:], identity[:])
         bias = keep.tile([P, TILES], F32, name="bias")
-        nc.scalar.copy(bias[:], bias_turned[:, 0:TILES])
+        nc.scalar.copy(bias[:], bias_turned[:, P - TILES :])
 
         picked_scales = keep.tile([P, S], U8, name="picked_scales", align_bytes=64)
         nc.vector.tensor_copy(picked_scales[:], scale_rows[:].indirect(offsets[:]))
         words.append(keep.tile([P, N], I32, name="words1", tag="scale_rows_then_words", align_bytes=64))
+        nc.sync.dma_start(out=words[1][:, :LEAD], in_=w_rows[1][:, :LEAD])
         for q in range(4):
             nc.sync.dma_start(
                 out=planes[32 * q : 32 * q + 4].bitcast(I32),
-                in_=picked_scales[8 * q : 8 * q + 8, :].bitcast(I32),
+                in_=picked_scales[96 + 8 * q : 96 + 8 * q + 8, :].bitcast(I32),
             )
-        nc.sync.dma_start(out=words[1][:, :REACH], in_=w_rows[1][:, :REACH])
+        nc.sync.dma_start(out=words[1][:, LEAD:REACH], in_=w_rows[1][:, LEAD:REACH])
         nc.sync.dma_start(out=words[1][:, REACH:], in_=w_rows[1][:, REACH:])
 
         x_codes = []
         x_scales = []
         for o in range(PASSES):
             grouped = keep.tile([P, T, PACK], BF16, name=f"grouped{o}", align_bytes=64)
-            nc.vector.tensor_copy(grouped[:], x_raw[:, o].rearrange("p j t -> p t j"))
+            if o == 1:
+                nc.scalar.copy(grouped[:], x_raw[:, o].rearrange("p j t -> p t j"))
+            else:
+                nc.vector.tensor_copy(grouped[:], x_raw[:, o].rearrange("p j t -> p t j"))
             codes = keep.tile([P, T], U32, name=f"x_codes{o}", align_bytes=64)
             scales = keep.tile([P, T], U8, name=f"x_scales{o}", align_bytes=64)
             nc.vector.quantize_mx(

@@ -24,7 +24,6 @@ TILES = S // P
 HALF = S // 2
 LIST_ROWS = 16
 REACH = N - HALF
-LEAD = 512
 
 
 def tile_picked_neuron_lin_relu_srt_p_kernel(tc, w_words, w_scales, xT, b, offs, out):
@@ -62,13 +61,12 @@ def tile_picked_neuron_lin_relu_srt_p_kernel(tc, w_words, w_scales, xT, b, offs,
         picked_scales = keep.tile([P, S], U8, name="picked_scales", align_bytes=64)
         nc.vector.tensor_copy(picked_scales[:], scale_rows[:].indirect(offsets[:]))
         words.append(keep.tile([P, N], I32, name="words1", tag="scale_rows_then_words", align_bytes=64))
-        nc.sync.dma_start(out=words[1][:, :LEAD], in_=w_rows[1][:, :LEAD])
         for q in range(4):
             nc.sync.dma_start(
                 out=planes[32 * q : 32 * q + 4].bitcast(I32),
                 in_=picked_scales[96 + 8 * q : 96 + 8 * q + 8, :].bitcast(I32),
             )
-        nc.sync.dma_start(out=words[1][:, LEAD:REACH], in_=w_rows[1][:, LEAD:REACH])
+        nc.sync.dma_start(out=words[1][:, :REACH], in_=w_rows[1][:, :REACH])
         nc.sync.dma_start(out=words[1][:, REACH:], in_=w_rows[1][:, REACH:])
 
         x_codes = []

@@ -61,7 +61,7 @@ def tile_picked_neuron_lin_relu_srt_p_kernel(tc, w_words, w_scales, xT, b, offs,
         picked_scales = keep.tile([P, S], U8, name="picked_scales", align_bytes=64)
         nc.vector.tensor_copy(picked_scales[:], scale_rows[:].indirect(offsets[:]))
         words.append(keep.tile([P, N], I32, name="words1", tag="scale_rows_then_words", align_bytes=64))
-        for q in range(4):
+        for q in (0, 2, 1, 3):
             nc.sync.dma_start(
                 out=planes[32 * q : 32 * q + 4].bitcast(I32),
                 in_=picked_scales[96 + 8 * q : 96 + 8 * q + 8, :].bitcast(I32),
@@ -109,8 +109,11 @@ def tile_picked_neuron_lin_relu_srt_p_kernel(tc, w_words, w_scales, xT, b, offs,
         for m in range(TILES):
             result = keep.tile([P, T], F32, name=f"result{m}")
             for bank, (lo, hi) in zip(acc[m], spans[m]):
-                if lo == 0:
+                if (m == 0 if m < TILES // 2 else lo == 0):
                     nc.scalar.activation(result[:, lo:hi], bank[:], ACT.Relu, bias=bias[:, m : m + 1])
                 else:
                     nc.vector.tensor_scalar(result[:, lo:hi], bank[:], bias[:, m : m + 1], 0.0, ALU.add, ALU.max)
-            nc.sync.dma_start(out=out[m * P : (m + 1) * P, :], in_=result[:])
+                if m == 0:
+                    nc.sync.dma_start(out=out[:P, lo:hi], in_=result[:, lo:hi])
+            if m > 0:
+                nc.sync.dma_start(out=out[m * P : (m + 1) * P, :], in_=result[:])

@@ -1,7 +1,6 @@
 from contextlib import ExitStack
 
 import concourse.mybir as mybir
-from concourse.masks import make_identity
 
 K, T, S, N = 1024, 256, 512, 2048
 FLOPS = 2 * K * T * S
@@ -24,49 +23,45 @@ TILES = S // P
 HALF = S // 2
 LIST_ROWS = 16
 REACH = N - HALF
+BLOCK = 32
+SPACING = BLOCK // TILES
 
 
 def tile_picked_neuron_lin_relu_srt_p_kernel(tc, w_words, w_scales, xT, b, offs, out):
     nc = tc.nc
     with ExitStack() as ctx:
         keep = ctx.enter_context(tc.tile_pool(name="keep", bufs=1))
+        reused = ctx.enter_context(tc.tile_pool(name="reused", bufs=1))
         psum = ctx.enter_context(tc.psum_pool(name="psum", bufs=1))
 
         offsets = keep.tile([P, S // LIST_ROWS], U16, name="offsets")
         x_raw = keep.tile([P, PASSES, PACK, T], F32, name="x_raw")
-        scale_rows = keep.tile([P, N], U8, name="scale_rows", tag="scale_rows_then_words", align_bytes=64)
+        scale_rows = reused.tile([P, N], U8, name="scale_rows", offset=0, align_bytes=64)
         words = [keep.tile([P, N], I32, name="words0", align_bytes=64)]
         planes = keep.tile([P, PASSES, S], U8, name="planes", align_bytes=64)
-        bias_rows = keep.tile([P, P], F32, name="bias_rows")
-        identity = keep.tile([P, P], F32, name="identity")
 
-        make_identity(nc, identity[:])
-        nc.vector.memset(bias_rows[: P - TILES, :], 0.0)
         nc.vector.memset(scale_rows[:96, :].bitcast(I32), 0)
         nc.vector.memset(planes[:].bitcast(I32), 0)
 
         x_rows = xT.rearrange("(o p j) t -> p o j t", o=PASSES, j=PACK)
         w_rows = [w_words[o].rearrange("p n r -> p (n r)").bitcast(I32) for o in range(PASSES)]
-        nc.sync.dma_start(offsets[:], offs)
         nc.sync.dma_start(out=scale_rows[96:, :].bitcast(I32), in_=w_scales.bitcast(I32).rearrange("o q n -> q o n"))
+        nc.sync.dma_start(offsets[:], offs)
         nc.sync.dma_start(out=x_raw[:], in_=x_rows)
         nc.sync.dma_start(out=words[0][:], in_=w_rows[0])
-        nc.scalar.dma_start(out=bias_rows[P - TILES :, :], in_=b.rearrange("(m p) one -> m (p one)", p=P))
-
-        bias_turned = psum.tile([P, P], F32, name="bias_turned", tag="acc3_128")
-        nc.tensor.transpose(bias_turned[:], bias_rows[:], identity[:])
-        bias = keep.tile([P, TILES], F32, name="bias")
-        nc.scalar.copy(bias[:], bias_turned[:, P - TILES :])
 
         picked_scales = keep.tile([P, S], U8, name="picked_scales", align_bytes=64)
         nc.vector.tensor_copy(picked_scales[:], scale_rows[:].indirect(offsets[:]))
-        words.append(keep.tile([P, N], I32, name="words1", tag="scale_rows_then_words", align_bytes=64))
+        bias_rows = reused.tile([P, BLOCK], F32, name="bias_rows", offset=0, align_bytes=64)
+        words.append(reused.tile([P, N], I32, name="words1", offset=4 * BLOCK, align_bytes=64))
+        nc.gpsimd.memset(bias_rows[:], 0.0)
         for q in (0, 2, 1, 3):
             nc.sync.dma_start(
                 out=planes[32 * q : 32 * q + 4].bitcast(I32),
                 in_=picked_scales[96 + 8 * q : 96 + 8 * q + 8, :].bitcast(I32),
             )
         nc.sync.dma_start(out=words[1][:, :REACH], in_=w_rows[1][:, :REACH])
+        nc.sync.dma_start(out=bias_rows[0:P:SPACING, :], in_=b.rearrange("(m q j) one -> q m (j one)", m=TILES, j=BLOCK))
         nc.sync.dma_start(out=words[1][:, REACH:], in_=w_rows[1][:, REACH:])
 
         x_codes = []
@@ -87,8 +82,11 @@ def tile_picked_neuron_lin_relu_srt_p_kernel(tc, w_words, w_scales, xT, b, offs,
 
         spans = [[(0, T // 2), (T // 2, T)] for m in range(TILES)]
         acc = [[psum.tile([P, hi - lo], F32, name=f"acc{m}_{lo}", tag=f"acc{m}_{lo}") for lo, hi in spans[m]] for m in range(TILES)]
+        bias = keep.tile([P, BLOCK], F32, name="bias", align_bytes=64)
         for o in range(PASSES):
             for h in range(2):
+                if (o, h) == (1, 1):
+                    nc.vector.transpose(bias[:], bias_rows[:])
                 picked = keep.tile([P, HALF], U32, name=f"picked{o}_{h}", align_bytes=64)
                 reach = REACH if (o, h) == (1, 0) else N
                 cols = slice(h * HALF // LIST_ROWS, (h + 1) * HALF // LIST_ROWS)
@@ -107,12 +105,15 @@ def tile_picked_neuron_lin_relu_srt_p_kernel(tc, w_words, w_scales, xT, b, offs,
                         )
 
         for m in range(TILES):
-            result = keep.tile([P, T], F32, name=f"result{m}")
+            if m == 1:
+                result = reused.tile([P, T], F32, name="result1", offset=4 * BLOCK, align_bytes=64)
+            else:
+                result = keep.tile([P, T], F32, name=f"result{m}")
             for bank, (lo, hi) in zip(acc[m], spans[m]):
                 if (m == 0 if m < TILES // 2 else lo == 0):
-                    nc.scalar.activation(result[:, lo:hi], bank[:], ACT.Relu, bias=bias[:, m : m + 1])
+                    nc.scalar.activation(result[:, lo:hi], bank[:], ACT.Relu, bias=bias[:, SPACING * m : SPACING * m + 1])
                 else:
-                    nc.vector.tensor_scalar(result[:, lo:hi], bank[:], bias[:, m : m + 1], 0.0, ALU.add, ALU.max)
+                    nc.vector.tensor_scalar(result[:, lo:hi], bank[:], bias[:, SPACING * m : SPACING * m + 1], 0.0, ALU.add, ALU.max)
                 if m == 0:
                     nc.sync.dma_start(out=out[:P, lo:hi], in_=result[:, lo:hi])
             if m > 0:

@@ -69,7 +69,7 @@ def tile_picked_neuron_lin_relu_srt_p_kernel(tc, w_words, w_scales, xT, b, offs,
         for o in range(PASSES):
             grouped = keep.tile([P, T, PACK], BF16, name=f"grouped{o}", align_bytes=64)
             if o == 1:
-                nc.scalar.copy(grouped[:], x_raw[:, o].rearrange("p j t -> p t j"))
+                nc.scalar.activation(grouped[:], x_raw[:, o].rearrange("p j t -> p t j"), ACT.Identity)
             else:
                 nc.vector.tensor_copy(grouped[:], x_raw[:, o].rearrange("p j t -> p t j"))
             codes = keep.tile([P, T], U32, name=f"x_codes{o}", align_bytes=64)

@@ -80,7 +80,7 @@ def tile_picked_neuron_lin_relu_srt_p_kernel(tc, w_words, w_scales, xT, b, offs,
             x_codes.append(codes)
             x_scales.append(scales)
 
-        spans = [[(0, T // 2), (T // 2, T)] for m in range(TILES)]
+        spans = [[(0, T)] if m == 1 else [(0, T // 2), (T // 2, T)] for m in range(TILES)]
         acc = [[psum.tile([P, hi - lo], F32, name=f"acc{m}_{lo}", tag=f"acc{m}_{lo}") for lo, hi in spans[m]] for m in range(TILES)]
         bias = keep.tile([P, BLOCK], F32, name="bias", align_bytes=64)
         for o in range(PASSES):

@@ -25,6 +25,7 @@ LIST_ROWS = 16
 REACH = N - HALF
 BLOCK = 32
 SPACING = BLOCK // TILES
+BURST = 256
 
 
 def tile_picked_neuron_lin_relu_srt_p_kernel(tc, w_words, w_scales, xT, b, offs, out):
@@ -34,11 +35,11 @@ def tile_picked_neuron_lin_relu_srt_p_kernel(tc, w_words, w_scales, xT, b, offs,
         reused = ctx.enter_context(tc.tile_pool(name="reused", bufs=1))
         psum = ctx.enter_context(tc.psum_pool(name="psum", bufs=1))
 
-        offsets = keep.tile([P, S // LIST_ROWS], U16, name="offsets")
-        x_raw = keep.tile([P, PASSES, PACK, T], F32, name="x_raw")
-        scale_rows = reused.tile([P, N], U8, name="scale_rows", offset=0, align_bytes=64)
-        words = [keep.tile([P, N], I32, name="words0", align_bytes=64)]
-        planes = keep.tile([P, PASSES, S], U8, name="planes", align_bytes=64)
+        offsets = keep.tile([P, S // LIST_ROWS], U16, name="offsets", align_bytes=BURST)
+        x_raw = keep.tile([P, PASSES, PACK, T], F32, name="x_raw", align_bytes=BURST)
+        scale_rows = reused.tile([P, N], U8, name="scale_rows", offset=0, align_bytes=BURST)
+        words = [keep.tile([P, N], I32, name="words0", align_bytes=BURST)]
+        planes = keep.tile([P, PASSES, S], U8, name="planes", align_bytes=BURST)
 
         nc.vector.memset(scale_rows[:96, :].bitcast(I32), 0)
         nc.vector.memset(planes[:].bitcast(I32), 0)
@@ -50,10 +51,10 @@ def tile_picked_neuron_lin_relu_srt_p_kernel(tc, w_words, w_scales, xT, b, offs,
         nc.sync.dma_start(out=x_raw[:], in_=x_rows)
         nc.sync.dma_start(out=words[0][:], in_=w_rows[0])
 
-        picked_scales = keep.tile([P, S], U8, name="picked_scales", align_bytes=64)
+        picked_scales = keep.tile([P, S], U8, name="picked_scales", align_bytes=BURST)
         nc.vector.tensor_copy(picked_scales[:], scale_rows[:].indirect(offsets[:]))
-        bias_rows = reused.tile([P, BLOCK], F32, name="bias_rows", offset=0, align_bytes=64)
-        words.append(reused.tile([P, N], I32, name="words1", offset=4 * BLOCK, align_bytes=64))
+        bias_rows = reused.tile([P, BLOCK], F32, name="bias_rows", offset=0, align_bytes=BURST)
+        words.append(reused.tile([P, N], I32, name="words1", offset=BURST, align_bytes=BURST))
         nc.gpsimd.memset(bias_rows[:], 0.0)
         for q in (0, 2, 1, 3):
             nc.sync.dma_start(
@@ -67,13 +68,13 @@ def tile_picked_neuron_lin_relu_srt_p_kernel(tc, w_words, w_scales, xT, b, offs,
         x_codes = []
         x_scales = []
         for o in range(PASSES):
-            grouped = keep.tile([P, T, PACK], BF16, name=f"grouped{o}", align_bytes=64)
+            grouped = keep.tile([P, T, PACK], BF16, name=f"grouped{o}", align_bytes=BURST)
             if o == 1:
                 nc.scalar.activation(grouped[:], x_raw[:, o].rearrange("p j t -> p t j"), ACT.Identity)
             else:
                 nc.vector.tensor_copy(grouped[:], x_raw[:, o].rearrange("p j t -> p t j"))
-            codes = keep.tile([P, T], U32, name=f"x_codes{o}", align_bytes=64)
-            scales = keep.tile([P, T], U8, name=f"x_scales{o}", align_bytes=64)
+            codes = keep.tile([P, T], U32, name=f"x_codes{o}", align_bytes=BURST)
+            scales = keep.tile([P, T], U8, name=f"x_scales{o}", align_bytes=BURST)
             nc.vector.quantize_mx(
                 out=codes[:].bitcast(FP8X4), scales=scales[:], in_=grouped[:].rearrange("p t j -> p (t j)")
             )
@@ -82,12 +83,12 @@ def tile_picked_neuron_lin_relu_srt_p_kernel(tc, w_words, w_scales, xT, b, offs,
 
         spans = [[(0, T)] if m == 1 else [(0, T // 2), (T // 2, T)] for m in range(TILES)]
         acc = [[psum.tile([P, hi - lo], F32, name=f"acc{m}_{lo}", tag=f"acc{m}_{lo}") for lo, hi in spans[m]] for m in range(TILES)]
-        bias = keep.tile([P, BLOCK], F32, name="bias", align_bytes=64)
+        bias = keep.tile([P, BLOCK], F32, name="bias", align_bytes=BURST)
         for o in range(PASSES):
             for h in range(2):
                 if (o, h) == (1, 1):
                     nc.vector.transpose(bias[:], bias_rows[:])
-                picked = keep.tile([P, HALF], U32, name=f"picked{o}_{h}", align_bytes=64)
+                picked = keep.tile([P, HALF], U32, name=f"picked{o}_{h}", align_bytes=BURST)
                 reach = REACH if (o, h) == (1, 0) else N
                 cols = slice(h * HALF // LIST_ROWS, (h + 1) * HALF // LIST_ROWS)
                 nc.vector.tensor_copy(picked[:], words[o][:, :reach].bitcast(U32).indirect(offsets[:, cols]))
@@ -106,9 +107,9 @@ def tile_picked_neuron_lin_relu_srt_p_kernel(tc, w_words, w_scales, xT, b, offs,
 
         for m in range(TILES):
             if m == 1:
-                result = reused.tile([P, T], F32, name="result1", offset=4 * BLOCK, align_bytes=64)
+                result = reused.tile([P, T], F32, name="result1", offset=BURST, align_bytes=BURST)
             else:
-                result = keep.tile([P, T], F32, name=f"result{m}")
+                result = keep.tile([P, T], F32, name=f"result{m}", align_bytes=BURST)
             for bank, (lo, hi) in zip(acc[m], spans[m]):
                 if (m == 0 if m < TILES // 2 else lo == 0):
                     nc.scalar.activation(result[:, lo:hi], bank[:], ACT.Relu, bias=bias[:, SPACING * m : SPACING * m + 1])

@@ -85,15 +85,16 @@ def tile_picked_neuron_lin_relu_srt_p_kernel(tc, w_words, w_scales, xT, b, offs,
         acc = [[psum.tile([P, hi - lo], F32, name=f"acc{m}_{lo}", tag=f"acc{m}_{lo}") for lo, hi in spans[m]] for m in range(TILES)]
         bias = keep.tile([P, BLOCK], F32, name="bias", align_bytes=BURST)
         for o in range(PASSES):
-            for h in range(2):
+            width = P if o == 0 else HALF
+            for h in range(S // width):
                 if (o, h) == (1, 1):
                     nc.vector.transpose(bias[:], bias_rows[:])
-                picked = keep.tile([P, HALF], U32, name=f"picked{o}_{h}", align_bytes=BURST)
+                picked = keep.tile([P, width], U32, name=f"picked{o}_{h}", align_bytes=BURST)
                 reach = REACH if (o, h) == (1, 0) else N
-                cols = slice(h * HALF // LIST_ROWS, (h + 1) * HALF // LIST_ROWS)
+                cols = slice(h * width // LIST_ROWS, (h + 1) * width // LIST_ROWS)
                 nc.vector.tensor_copy(picked[:], words[o][:, :reach].bitcast(U32).indirect(offsets[:, cols]))
-                for i in range(HALF // P):
-                    m = h * (HALF // P) + i
+                for i in range(width // P):
+                    m = h * (width // P) + i
                     for bank, (lo, hi) in zip(acc[m], spans[m]):
                         nc.tensor.matmul_mx(
                             out=bank[:],

@@ -33,6 +33,7 @@ def tile_picked_neuron_lin_relu_srt_p_kernel(tc, w_words, w_scales, xT, b, offs,
     with ExitStack() as ctx:
         keep = ctx.enter_context(tc.tile_pool(name="keep", bufs=1))
         reused = ctx.enter_context(tc.tile_pool(name="reused", bufs=1))
+        held = ctx.enter_context(tc.tile_pool(name="held", bufs=1))
         psum = ctx.enter_context(tc.psum_pool(name="psum", bufs=1))
 
         offsets = keep.tile([P, S // LIST_ROWS], U16, name="offsets", align_bytes=BURST)
@@ -67,13 +68,17 @@ def tile_picked_neuron_lin_relu_srt_p_kernel(tc, w_words, w_scales, xT, b, offs,
 
         x_codes = []
         x_scales = []
-        for o in range(PASSES):
+
+        def quantise(o):
             grouped = keep.tile([P, T, PACK], BF16, name=f"grouped{o}", align_bytes=BURST)
             if o == 1:
                 nc.scalar.activation(grouped[:], x_raw[:, o].rearrange("p j t -> p t j"), ACT.Identity)
             else:
                 nc.vector.tensor_copy(grouped[:], x_raw[:, o].rearrange("p j t -> p t j"))
-            codes = keep.tile([P, T], U32, name=f"x_codes{o}", align_bytes=BURST)
+            if o == 1:
+                codes = held.tile([P, T], U32, name="x_codes1", offset=0, align_bytes=BURST)
+            else:
+                codes = keep.tile([P, T], U32, name="x_codes0", align_bytes=BURST)
             scales = keep.tile([P, T], U8, name=f"x_scales{o}", align_bytes=BURST)
             nc.vector.quantize_mx(
                 out=codes[:].bitcast(FP8X4), scales=scales[:], in_=grouped[:].rearrange("p t j -> p (t j)")
@@ -85,11 +90,26 @@ def tile_picked_neuron_lin_relu_srt_p_kernel(tc, w_words, w_scales, xT, b, offs,
         acc = [[psum.tile([P, hi - lo], F32, name=f"acc{m}_{lo}", tag=f"acc{m}_{lo}") for lo, hi in spans[m]] for m in range(TILES)]
         bias = keep.tile([P, BLOCK], F32, name="bias", align_bytes=BURST)
         for o in range(PASSES):
+            quantise(o)
+            if o == 1:
+                unread = psum.tile([P, P], F32, name="unread", tag="unread")
+                nc.tensor.matmul_mx(
+                    out=unread[:],
+                    lhsT=x_codes[1][:, :P].bitcast(FP8X4),
+                    lhsT_scale=x_scales[1][:, :P],
+                    rhs=x_codes[1][:, P:].bitcast(FP8X4),
+                    rhs_scale=x_scales[1][:, P:],
+                    start=True,
+                    stop=True,
+                )
             width = P if o == 0 else HALF
             for h in range(S // width):
                 if (o, h) == (1, 1):
                     nc.vector.transpose(bias[:], bias_rows[:])
-                picked = keep.tile([P, width], U32, name=f"picked{o}_{h}", align_bytes=BURST)
+                if (o, h) == (0, 0):
+                    picked = held.tile([P, width], U32, name="picked0_0", offset=0, align_bytes=BURST)
+                else:
+                    picked = keep.tile([P, width], U32, name=f"picked{o}_{h}", align_bytes=BURST)
                 reach = REACH if (o, h) == (1, 0) else N
                 cols = slice(h * width // LIST_ROWS, (h + 1) * width // LIST_ROWS)
                 nc.vector.tensor_copy(picked[:], words[o][:, :reach].bitcast(U32).indirect(offsets[:, cols]))

@@ -26,6 +26,7 @@ REACH = N - HALF
 BLOCK = 32
 SPACING = BLOCK // TILES
 BURST = 256
+WARM_UP = (128, 64)
 
 
 def tile_picked_neuron_lin_relu_srt_p_kernel(tc, w_words, w_scales, xT, b, offs, out):
@@ -92,16 +93,17 @@ def tile_picked_neuron_lin_relu_srt_p_kernel(tc, w_words, w_scales, xT, b, offs,
         for o in range(PASSES):
             quantise(o)
             if o == 1:
-                unread = psum.tile([P, P], F32, name="unread", tag="unread")
-                nc.tensor.matmul_mx(
-                    out=unread[:],
-                    lhsT=x_codes[1][:, :P].bitcast(FP8X4),
-                    lhsT_scale=x_scales[1][:, :P],
-                    rhs=x_codes[1][:, P:].bitcast(FP8X4),
-                    rhs_scale=x_scales[1][:, P:],
-                    start=True,
-                    stop=True,
-                )
+                unread = psum.tile([P, sum(WARM_UP)], F32, name="unread", tag="unread")
+                for lo, n in zip((0, WARM_UP[0]), WARM_UP):
+                    nc.tensor.matmul_mx(
+                        out=unread[:, lo : lo + n],
+                        lhsT=x_codes[1][:, :P].bitcast(FP8X4),
+                        lhsT_scale=x_scales[1][:, :P],
+                        rhs=x_codes[1][:, lo : lo + n].bitcast(FP8X4),
+                        rhs_scale=x_scales[1][:, lo : lo + n],
+                        start=True,
+                        stop=True,
+                    )
             width = P if o == 0 else HALF
             for h in range(S // width):
                 if (o, h) == (1, 1):

@@ -26,7 +26,6 @@ REACH = N - HALF
 BLOCK = 32
 SPACING = BLOCK // TILES
 BURST = 256
-WARM_UP = (128, 64)
 
 
 def tile_picked_neuron_lin_relu_srt_p_kernel(tc, w_words, w_scales, xT, b, offs, out):
@@ -92,18 +91,6 @@ def tile_picked_neuron_lin_relu_srt_p_kernel(tc, w_words, w_scales, xT, b, offs,
         bias = keep.tile([P, BLOCK], F32, name="bias", align_bytes=BURST)
         for o in range(PASSES):
             quantise(o)
-            if o == 1:
-                unread = psum.tile([P, sum(WARM_UP)], F32, name="unread", tag="unread")
-                for lo, n in zip((0, WARM_UP[0]), WARM_UP):
-                    nc.tensor.matmul_mx(
-                        out=unread[:, lo : lo + n],
-                        lhsT=x_codes[1][:, :P].bitcast(FP8X4),
-                        lhsT_scale=x_scales[1][:, :P],
-                        rhs=x_codes[1][:, lo : lo + n].bitcast(FP8X4),
-                        rhs_scale=x_scales[1][:, lo : lo + n],
-                        start=True,
-                        stop=True,
-                    )
             width = P if o == 0 else HALF
             for h in range(S // width):
                 if (o, h) == (1, 1):

from contextlib import ExitStack

import concourse.mybir as mybir

K, T, S, N = 1024, 256, 512, 2048
FLOPS = 2 * K * T * S

F32 = mybir.dt.float32
BF16 = mybir.dt.bfloat16
I32 = mybir.dt.int32
U32 = mybir.dt.uint32
U16 = mybir.dt.uint16
U8 = mybir.dt.uint8
FP8X4 = mybir.dt.float8_e4m3fn_x4
ACT = mybir.ActivationFunctionType
ALU = mybir.AluOpType

P = 128
PACK = 4
K_PASS = P * PACK
PASSES = K // K_PASS
TILES = S // P
HALF = S // 2
LIST_ROWS = 16
REACH = N - HALF
BLOCK = 32
SPACING = BLOCK // TILES
BURST = 256


def tile_picked_neuron_lin_relu_srt_p_kernel(tc, w_words, w_scales, xT, b, offs, out):
    nc = tc.nc
    with ExitStack() as ctx:
        keep = ctx.enter_context(tc.tile_pool(name="keep", bufs=1))
        reused = ctx.enter_context(tc.tile_pool(name="reused", bufs=1))
        held = ctx.enter_context(tc.tile_pool(name="held", bufs=1))
        psum = ctx.enter_context(tc.psum_pool(name="psum", bufs=1))

        offsets = keep.tile([P, S // LIST_ROWS], U16, name="offsets", align_bytes=BURST)
        x_raw = keep.tile([P, PASSES, PACK, T], F32, name="x_raw", align_bytes=BURST)
        scale_rows = reused.tile([P, N], U8, name="scale_rows", offset=0, align_bytes=BURST)
        words = [keep.tile([P, N], I32, name="words0", align_bytes=BURST)]
        planes = keep.tile([P, PASSES, S], U8, name="planes", align_bytes=BURST)

        nc.vector.memset(scale_rows[:96, :].bitcast(I32), 0)
        nc.vector.memset(planes[:].bitcast(I32), 0)

        x_rows = xT.rearrange("(o p j) t -> p o j t", o=PASSES, j=PACK)
        w_rows = [w_words[o].rearrange("p n r -> p (n r)").bitcast(I32) for o in range(PASSES)]
        nc.sync.dma_start(out=scale_rows[96:, :].bitcast(I32), in_=w_scales.bitcast(I32).rearrange("o q n -> q o n"))
        nc.sync.dma_start(offsets[:], offs)
        nc.sync.dma_start(out=x_raw[:], in_=x_rows)
        nc.sync.dma_start(out=words[0][:], in_=w_rows[0])

        picked_scales = keep.tile([P, S], U8, name="picked_scales", align_bytes=BURST)
        nc.vector.tensor_copy(picked_scales[:], scale_rows[:].indirect(offsets[:]))
        bias_rows = reused.tile([P, BLOCK], F32, name="bias_rows", offset=0, align_bytes=BURST)
        words.append(reused.tile([P, N], I32, name="words1", offset=BURST, align_bytes=BURST))
        nc.gpsimd.memset(bias_rows[:], 0.0)
        for q in (0, 2, 1, 3):
            nc.sync.dma_start(
                out=planes[32 * q : 32 * q + 4].bitcast(I32),
                in_=picked_scales[96 + 8 * q : 96 + 8 * q + 8, :].bitcast(I32),
            )
        nc.sync.dma_start(out=words[1][:, :REACH], in_=w_rows[1][:, :REACH])
        nc.sync.dma_start(out=bias_rows[0:P:SPACING, :], in_=b.rearrange("(m q j) one -> q m (j one)", m=TILES, j=BLOCK))
        nc.sync.dma_start(out=words[1][:, REACH:], in_=w_rows[1][:, REACH:])

        x_codes = []
        x_scales = []

        def quantise(o):
            grouped = keep.tile([P, T, PACK], BF16, name=f"grouped{o}", align_bytes=BURST)
            if o == 1:
                nc.scalar.activation(grouped[:], x_raw[:, o].rearrange("p j t -> p t j"), ACT.Identity)
            else:
                nc.vector.tensor_copy(grouped[:], x_raw[:, o].rearrange("p j t -> p t j"))
            if o == 1:
                codes = held.tile([P, T], U32, name="x_codes1", offset=0, align_bytes=BURST)
            else:
                codes = keep.tile([P, T], U32, name="x_codes0", align_bytes=BURST)
            scales = keep.tile([P, T], U8, name=f"x_scales{o}", align_bytes=BURST)
            nc.vector.quantize_mx(
                out=codes[:].bitcast(FP8X4), scales=scales[:], in_=grouped[:].rearrange("p t j -> p (t j)")
            )
            x_codes.append(codes)
            x_scales.append(scales)

        spans = [[(0, T)] if m == 1 else [(0, T // 2), (T // 2, T)] for m in range(TILES)]
        acc = [[psum.tile([P, hi - lo], F32, name=f"acc{m}_{lo}", tag=f"acc{m}_{lo}") for lo, hi in spans[m]] for m in range(TILES)]
        bias = keep.tile([P, BLOCK], F32, name="bias", align_bytes=BURST)
        for o in range(PASSES):
            quantise(o)
            width = P if o == 0 else HALF
            for h in range(S // width):
                if (o, h) == (1, 1):
                    nc.vector.transpose(bias[:], bias_rows[:])
                if (o, h) == (0, 0):
                    picked = held.tile([P, width], U32, name="picked0_0", offset=0, align_bytes=BURST)
                else:
                    picked = keep.tile([P, width], U32, name=f"picked{o}_{h}", align_bytes=BURST)
                reach = REACH if (o, h) == (1, 0) else N
                cols = slice(h * width // LIST_ROWS, (h + 1) * width // LIST_ROWS)
                nc.vector.tensor_copy(picked[:], words[o][:, :reach].bitcast(U32).indirect(offsets[:, cols]))
                for i in range(width // P):
                    m = h * (width // P) + i
                    for bank, (lo, hi) in zip(acc[m], spans[m]):
                        nc.tensor.matmul_mx(
                            out=bank[:],
                            lhsT=picked[:, i * P : (i + 1) * P].bitcast(FP8X4),
                            lhsT_scale=planes[:, o, m * P : (m + 1) * P],
                            rhs=x_codes[o][:, lo:hi].bitcast(FP8X4),
                            rhs_scale=x_scales[o][:, lo:hi],
                            start=(o == 0),
                            stop=(o == PASSES - 1),
                        )

        for m in range(TILES):
            if m == 1:
                result = reused.tile([P, T], F32, name="result1", offset=BURST, align_bytes=BURST)
            else:
                result = keep.tile([P, T], F32, name=f"result{m}", align_bytes=BURST)
            for bank, (lo, hi) in zip(acc[m], spans[m]):
                if (m == 0 if m < TILES // 2 else lo == 0):
                    nc.scalar.activation(result[:, lo:hi], bank[:], ACT.Relu, bias=bias[:, SPACING * m : SPACING * m + 1])
                else:
                    nc.vector.tensor_scalar(result[:, lo:hi], bank[:], bias[:, SPACING * m : SPACING * m + 1], 0.0, ALU.add, ALU.max)
                if m == 0:
                    nc.sync.dma_start(out=out[:P, lo:hi], in_=result[:, lo:hi])
            if m > 0:
                nc.sync.dma_start(out=out[m * P : (m + 1) * P, :], in_=result[:])
